import numpy as np, ml_dtypes
CORES = [40,41,42,43,44,45,46,47]
N = 8
import mx_ref
BF = ml_dtypes.bfloat16
def gcols(t, e):
    v = np.concatenate([t.reshape(8, 16, -1, 4), np.zeros((8, 16, 1, 4), BF)], axis=2)
    return np.ascontiguousarray(np.stack([v[g][:, e[g]] for g in range(8)])).reshape(128, -1)
def tile(rs):
    return np.stack(rs, axis=2).reshape(128, -1).astype(BF)
def pick(q, e):
    c = np.concatenate([q[0].reshape(128, -1, 4), np.zeros((128, 1, 4), np.uint8)], axis=1); s = np.concatenate([q[1], np.ones((16, 1), np.uint8)], axis=1)
    return (np.ascontiguousarray(c[:, e].reshape(128, -1)), np.ascontiguousarray(s[:, e]))
def join(*qs):
    return (np.concatenate([q[0] for q in qs], axis=1), np.concatenate([q[1] for q in qs], axis=1))
def put(q, e, v):
    c, s = q[0].reshape(128, -1, 4).copy(), q[1].copy(); c[:, e] = v[0].reshape(128, -1, 4); s[:, e] = v[1]
    return (c.reshape(128, -1), s)
def pk(c, s):
    return (np.ascontiguousarray(c), mx_ref.live(s))
def emit(q):
    return q[0], q[1]
def packed(v, rng):
    q = [mx_ref.quantize(np.ascontiguousarray(v[r])) for r in range(N)]
    return np.stack([a for a, b in q]), np.stack([mx_ref.plane(b, rng) for a, b in q])
def values_of_codes():
    e, c = np.zeros((128, 128, 4), np.float32), np.zeros((128, 2, 4), np.uint8)
    e[np.arange(128), np.arange(128), 0] = 1
    c[:127, :, 0] = np.arange(256).reshape(2, 128).T[:127]
    return mx_ref.matmul(mx_ref.quantize(e.reshape(128, 512).astype(BF)), (c.reshape(128, 8), np.full((16, 2), 127, np.uint8))).T.reshape(-1).astype(np.float64)
CODE_VALUE, SCALE_VALUE = values_of_codes(), 2.0 ** (np.arange(256) - 127.0)
def decode(q):
    return (CODE_VALUE[q[0]].reshape(16, 8, -1, 4) * SCALE_VALUE[q[1]][:, None, :, None] + 0.0).reshape(128, -1).astype(np.float32)
def f(rng, *shape):
    return mx_ref.flush((rng.standard_normal(shape, dtype=np.float32) * np.exp2(rng.integers(-2, 3, shape[:-1] + (1,)))).astype(BF))
def wide(rng, *shape, cols=0):
    v = rng.standard_normal(shape, dtype=np.float32) * np.exp2(rng.integers(-12, 13, shape)).astype(np.float32)
    if cols: v *= np.repeat(np.exp2(rng.integers(-cols, cols + 1, shape[:-2] + (1, shape[-1] // 4))) * (rng.random(shape[:-2] + (1, shape[-1] // 4)) > 0.0625), 4, axis=-1).astype(np.float32)
    return mx_ref.flush(v.astype(BF))
C, A, STEP = 256, 16, [1, 2]
def big(v):
    v = v.astype(np.float32)
    v[np.abs(v) < np.float32(2.0 ** -16)] = 0
    return v.astype(BF)
def numbers_of(rng):
    return {"x": big(f(rng, N, 128, 4 * C)), "u": np.array(f(rng, N, 128, 512)), "v": np.array(f(rng, N, 128, 512))}
def layers(rng):
    return big(rng.random((N, 128, 2048), dtype=np.float32) * 2 - 1).reshape(N, 8, 16, 4, 8, 16, 4)
def weights(rng, w):
    c, s = packed(np.ascontiguousarray(w).reshape(N, 128, 2048), rng)
    return {"wc": c, "ws": s}
def setup_inputs(rng):
    return {**numbers_of(rng), **weights(rng, layers(rng))}
def setup_inputs_ties(rng):
    d = numbers_of(rng)
    o = rng.permutation(N)
    x = d["x"].reshape(N, 8, 16, C, 4)
    x[:, :, :8] = 0
    x[:, :, 0, :, 0] = rng.integers(0, 4, (N, 8, C)).astype(np.float32).astype(BF)
    t = rng.integers(-1, 2, (N, 8, C, 3))
    t[o[0]] = -1
    t[o[0], :, A::A + 1, 0] = 1
    t[o[1]] = 1
    x[:, :, 1, :, :3] = t.astype(np.float32).astype(BF)
    u = d["u"].reshape(N, 128, 128, 4)
    for i in range(4): u[:, :, i::16] = 0
    for r in range(N):
        for h in range(0, 128, 16):
            u[r, h, h, 0] = 0.0 if r == o[0] else -1.0 if r == o[2] else 1.0
            for i in range(3): u[r, h + 1, h + 1 + i, i] = 1.0
    w = layers(rng)
    w[:, :, :, :, :, :8] = 0
    return {"x": x.reshape(N, 128, 4 * C), "u": u.reshape(N, 128, 512), "v": d["v"], **weights(rng, w)}
def setup_inputs_near(rng):
    d = numbers_of(rng)
    x = d["x"].astype(np.float32).reshape(N, 8, 16, C, 4)
    x[:, :, 0] = 0
    x[:, :, 8:] = 0
    u = d["u"].reshape(N, 128, 128, 4)
    for i in range(4): u[:, :, i::16] = 0
    o = rng.permutation(N) % 4
    for r in range(N):
        tiny = o[r] == 2
        k = 2.0 ** -30 if o[r] == 1 else 1.0
        if tiny:
            m = rng.integers(0, 8, (8, C))
            x[r, :, 8, :, 0] = (8 + m) * 2.0 ** -33
            x[r, :, 9, :, 0] = (15 - m) * 2.0 ** -33
        else:
            s = rng.integers(0, 16, (8, C))
            x[r, :, 0, :, 0] = 1.0 if o[r] == 0 else -1.0 if o[r] == 1 else rng.choice([-1.0, 1.0], (8, C))
            x[r, :, 8] = ((s[:, :, None] >> np.arange(4)) & 1) * np.exp2(np.arange(4) - 23.0)
            x[r, :, 11, :, 0] = 2.0 ** -10
        x[r, :, 12:15, :, 0] = rng.integers(-1, 2, (8, 3, C)) * (2.0 ** -30 if tiny else 2.0 ** -22)
        if o[r] in (0, 2):
            for g in rng.permutation(8)[:4]: x[r, g, 0, rng.integers(C), 1] = rng.choice([-1.0, 1.0]) * 2.0 ** 21
        for h in range(0, 128, 16):
            if tiny:
                u[r, h + 8, h, 0] = 1.125 * 2.0 ** -30
                u[r, h + 9, h, 0] = 2.0 ** -30
            else:
                u[r, h, h, 0] = k
                u[r, h + 8, h] = k
                u[r, h + 11, h, 0] = k
            if o[r] in (0, 2): u[r, h, h, 1] = 2.0 ** 9
            for i in range(3): u[r, h + 12 + i, h + 1 + i, 0] = 2.0 ** -30
    w = layers(rng)
    for i in [0, 8, 9, 10, 11, 12, 13, 14, 15]:
        w[:, :, i] = 0
        w[:, :, :, :, :, i] = 0
    return {"x": x.reshape(N, 128, 4 * C).astype(BF), "u": u.reshape(N, 128, 512), "v": d["v"], **weights(rng, w)}
def setup_inputs_ends(rng):
    d = numbers_of(rng)
    e = rng.permutation(N)
    top = e[0] ^ STEP[0] ^ STEP[1]
    mate = top ^ STEP[0]
    rest = [r for r in e[1:] if r not in (top, mate)]
    e = [e[0]] + rest[:N // 2 - 1] + [top, mate] + rest[N // 2 - 1:]
    c = rng.integers(8)
    x = np.zeros((N, 8, 16, C, 4), np.float32)
    u = d["u"].astype(np.float32).reshape(N, 8, 16, 128, 4)
    for i in range(4): u[:, :, :, i::16] = 0
    v = rng.choice([-1.0, 1.0], (N, 128, 512)).astype(np.float32)
    sign = lambda *s: rng.choice([-1.0, 1.0], s)
    for r in range(N):
        h = rng.permutation(8)
        if r in e[:N // 2]:
            t = sign(4, 1, 1, 1)
            if r == e[0]: t[:] = -1
            m = sign(8, 1, C, 1) * rng.choice([0.5, 0.75, 0.875, 1.0], (8, 1, C, 1))
            m[h[4:, None], 0, rng.permutation(C)[:64], 0] = -rng.choice([0.75, 0.875, 1.0], (4, 64))
            p = (m[h[4:]] > 0).all(axis=0)
            m[h[4]][p] *= -1
            m[h[:4]] = t
            x[r] = 2.0 ** 21 * m
            v[r] *= np.float32(2.0 ** 30)
            for n in range(8):
                g = h[n]
                if n < 4: u[r, h[:4], :, 16 * g] = -2.0 ** 30 * t[:, :, 0]
                if n in (2, 3): u[r, h[4:], :, 16 * g] = 2.0 ** 29 if n == 2 else 2.0 ** 30
                if n >= 4: u[r, h[4:], :, 16 * g] = 2.0 ** 30 * sign(4, 1, 1)
                for i in range(3): u[r, rng.choice(h[4:]), :, 16 * g + 1 + i] = 2.0 ** 30 * rng.choice([-1.0, 1.0])
        elif r == top:
            x[r] = 2.0 ** 21
            s = (rng.permutation(C)[:, None] >> np.arange(8)) & 1
            x[r, c, :2] = 2.0 ** 21 * (2.0 * s - 1.0).reshape(C, 2, 4).transpose(1, 0, 2)
            v[r] *= np.float32(2.0 ** 30)
            for n in range(8):
                g = h[n]
                u[r, :, :, 16 * g] = -2.0 ** 30 if n < 4 else 2.0 ** 30
                k = 4.0 * rng.permutation(2)[:, None] + rng.permutation(4)
                u[r, c, :2, 16 * g] *= np.exp2(-k).astype(np.float32)
        else:
            x[r, :, :8] = 2.0 ** -30 * sign(8, 1, C, 1)
            x[r, :, 8:] = sign(8, 1, C, 1)
            v[r] *= np.float32(2.0 ** -30)
            for n in range(8):
                g = h[n]
                if n >= 2: u[r, :, :8, 16 * g] = 2.0 ** -30 * sign(8, 1, 1)
                for i in range(3): u[r, rng.integers(8), :8, 16 * g + 1 + i] = 2.0 ** -30 * rng.choice([-1.0, 1.0])
    w = rng.choice([-1.0, 1.0], (N, 8, 16, 4, 8, 16, 4)).astype(np.float32)
    w[e[0]] = 1
    w[e[1]] = 0
    w[:, :, :8] = 0
    w[:, :, :, :, :, :8] = 0
    w[mate] = 1
    w[mate, c, :2] = 0
    return {"x": x.reshape(N, 128, 4 * C).astype(BF), "u": u.reshape(N, 128, 512).astype(BF), "v": v.astype(BF), **weights(rng, w.astype(BF))}
def setup_inputs_blocks(rng):
    d = numbers_of(rng)
    k = np.exp2(rng.integers(14, 19, (N, 8, 2, 1, C, 1)).astype(np.float64))
    s = (N, 8, 2, 8, C, 4)
    a = k * np.exp2(-rng.integers(8, 15, s).astype(np.float64)) * (1 + (2 * rng.integers(0, 64, s) + 1) * 2.0 ** -7) * rng.choice([-1.0, 1.0], s)
    a[:, :, :, 0, :, 0] = 1.96875 * k[:, :, :, 0, :, 0] * rng.choice([-1.0, 1.0], (N, 8, 2, C))
    u = d["u"].reshape(N, 128, 128, 4)
    e = rng.integers(N)
    for i in range(4): u[e, :, i::16] = 0
    w = layers(rng)
    w[:, :, ::8] = 0
    return {"x": a.astype(np.float32).reshape(N, 128, 4 * C).astype(BF), "u": u.reshape(N, 128, 512), "v": d["v"], **weights(rng, w)}
def setup_inputs_spread(rng):
    d = setup_inputs(rng)
    d["x"] = big(np.clip(wide(rng, N, 128, 4 * C, cols=6).astype(np.float32), -2.0 ** 21, 2.0 ** 21))
    return d
def check_inputs(d):
    b = []
    for k, top in (("x", 2.0 ** 21), ("u", 2.0 ** 30), ("v", 2.0 ** 30)):
        a = np.abs(d[k].astype(np.float32))
        if not (np.isfinite(a).all() and ((a == 0) | (a >= 2.0 ** -30) & (a <= top)).all()): b.append("a value of " + k)
    none, least, most = [emit(mx_ref.quantize(np.full((128, 16), k, np.float32).astype(BF)))[1][0, 0] for k in (0.0, 2.0 ** -30, 1.0)]
    for r in range(N):
        if ((d["wc"][r] == 0x7F) | (d["wc"][r] == 0xFF)).any(): b.append("wc: a code that is no number")
        s = mx_ref.live(d["ws"][r])
        if ((s != none) & ((s < least) | (s > most))).any(): b.append("ws: a scale out of range")
        elif (np.abs(decode(pk(d["wc"][r], d["ws"][r]))) > 1).any(): b.append("a number of W beyond 1")
    return b
def sources(s):
    order = np.argsort(-(s[::16] + np.float32(0.0)), axis=1, kind="stable")
    place = np.argsort(order, axis=1, kind="stable")
    kind = 1 * (s[1::16] > 0) + 2 * (s[2::16] > 0) + 4 * (s[3::16] > 0)
    used, j = np.zeros((C, 8), bool), np.arange(C)
    c = np.zeros((8, C), np.int64)
    for g in range(8):
        look = order[g][(place[(g + 1) % 8][:, None] + np.arange(A)) % C]
        new = ~used[j[:, None], kind[g][look]]
        c[g] = look[j, np.argmax(new, axis=1)]
        used[j, kind[g][c[g]]] = True
    return c
def reference(x, u, v, wc, ws):
    qu = [mx_ref.quantize(u[r]) for r in range(N)]
    lay = [[pick(pk(wc[r], ws[r]), np.arange(128 * b, 128 * b + 128)) for b in range(4)] for r in range(N)]
    now = [x[r] for r in range(N)]
    for h in STEP:
        q = [mx_ref.quantize(now[r]) for r in range(N)]
        own = [decode(q[r]) for r in range(N)]
        took = [sources(mx_ref.matmul(qu[r], q[r])) for r in range(N)]
        z = [mx_ref.quantize(gcols(own[r].astype(BF), took[r])) for r in range(N)]
        made = []
        for r in range(N):
            e = r ^ h
            back = mx_ref.quantize(tile([mx_ref.matmul(lay[e][b], z[r]) * np.float32(0.03125) + own[e][:, b::4] for b in range(4)]))
            first = np.full((8, C), -1)
            for g in range(8):
                for j in range(C - 1, -1, -1): first[g, took[r][g, j]] = j
            made.append((own[r] + gcols(decode(back).astype(BF), first).astype(np.float32)).astype(BF))
        now = made
    y, src = np.zeros((N, 128, C), np.float32), np.zeros((N, 8, C), np.float32)
    oc, osc = np.zeros((N, 128, 4 * C), np.uint8), np.zeros((N, 16, C), np.uint8)
    for r in range(N):
        p = mx_ref.quantize(now[r])
        y[r] = mx_ref.matmul(mx_ref.quantize(v[r]), p)
        src[r] = took[r]
        oc[r], osc[r] = emit(p)
    return {"y": y, "src": src, "oc": oc, "osc": osc}

@@ -1,0 +1,483 @@
+import numpy as np
+from concourse.bass import DstId, RemoteDMATransfer
+from concourse.mybir import dt, AluOpType, AxisListType, ActivationFunctionType
+
+OP = AluOpType
+AF = ActivationFunctionType
+BIG = 8e28
+K16 = 201326592.0
+EPS = 2.0 ** -19
+KE16, KE256 = 384.0, 6144.0
+W = 48
+STEP = [1, 2]
+
+F4, BF, I4, U2, CODE, U1 = "float32", "bfloat16", "int32", "uint16", "float8_e4m3fn_x4", "uint8"
+SCRATCH, PART = {}, {}
+
+
+def _add(dtype, **bufs):
+    for k, n in bufs.items():
+        SCRATCH[k] = ("sbuf", [128, n], dtype)
+
+
+def _pieces(base, dtype, **bufs):
+    at = 0
+    for k, n in bufs.items():
+        PART[k] = (base, at, n)
+        at += (n + 15) // 16 * 16
+    SCRATCH[base] = ("sbuf", [128, at], dtype)
+
+
+_add(BF, x0=1024, x1=1024, x2=1024, ut=512, vt=512, zz=512, kk=256, sg=256, cw=512, rot=512, ebig=2048, tc=1536,
+     mv=512, bt=1024, zs=272, z=256, d0=272, d1=272, tb=272, w0=272, w1=272, rt=512, tt=1024, ex=512, et=256, ets=256,
+     cm=4096, fo=1024, fp=1024, zt=1024, yt=1024, dy=1088, crow=256, eq=4096, pm=4096, fz=1024)
+_add(F4, ikf=256, maskd=256, hd=256, kz=256, kbi=256, lb=512, ab=256, sd=256, sx=256, junk=4096, fb=16 * W, so=16 * W,
+     srow=256, yout=256)
+_pieces("f4s", F4, pf=16, mask16=16, kcol=16, cb0=16, cb1=16, cb2=16, gm=8, ig8=8, iposf=50, nega=50, negb=50, negc=50, sig=48,
+        wt0=8, wt1=8, pos2=48, pos3=48, fbp=48, fbz=48, kai2=16, acc=16, acc2=16, rl=16, dah=16, dhh=16, ddb=16, dda=16)
+_pieces("i4s", I4, ip=1, pi=8, ikp=256, iposi=48, iu=8, kai=256, im=16)
+_pieces("u2s", U2, ul=8, l1=16, l2=16, l4=16)
+_add(U2, lc0=16, lc1=16, plc0=16, plc1=16)
+for _n, _w in (("uq", 128), ("ur", 128), ("vq", 128), ("wq", 512), ("xqa", 256), ("xqb", 256), ("xqc", 256), ("pxa", 256), ("pxb", 256),
+               ("cwq", 128), ("rotq", 128), ("eq_", 512), ("tcq", 384), ("mvq", 128), ("btq", 256), ("rtq", 128), ("ttq", 256),
+               ("exq", 128), ("zqa", 256), ("zqb", 256), ("yqa", 256), ("yqb", 256), ("pya", 256), ("pyb", 256)):
+    SCRATCH[_n] = ("sbuf", [128, _w], CODE)
+    SCRATCH[_n + "S"] = ("sbuf", [128, _w], U1)
+for _k in range(8):
+    SCRATCH["ps%d" % _k] = ("psum", [128, 512], F4)
+
+NDMA = 56
+SEMAPHORES = (["V", "A", "P", "G"] + ["d%d" % k for k in range(NDMA)] + [k + "%d" % r for k in ("rx", "lx", "rl", "ll") for r in (0, 1)]
+              + [k + "%d%d" % (r, h) for k in ("ry", "ly") for r in (0, 1) for h in (0, 1)])
+
+
+def rank_program(g, core, T, topo):
+    rank = T.rank_of(core)
+    if rank is None:
+        return
+    eng = {"V": g.vector, "A": g.scalar, "P": g.tensor, "G": g, "S": g.sync}
+    cnt = {"V": 0, "A": 0, "P": 0, "G": 0}
+    seen = {q: {} for q in eng}
+    log = {}
+    ndma = [0]
+    final = {}
+
+    def B(name, a=0, b=None, s=1):
+        if name in PART:
+            base, at, n = PART[name]
+            name, a, b = base, a + at, at + (n if b is None else b)
+        elif b is None:
+            b = SCRATCH[name][1][1]
+        ap = T[name][:, a:b] if s == 1 else T[name][:, a:b:s]
+        return (ap, name, a, b, s)
+
+    def U8(v):
+        return (v[0].bitcast(dt.uint8),) + v[1:]
+
+    def clash(u, v):
+        if u[3] <= v[2] or v[3] <= u[2]:
+            return False
+        return not (u[4] == v[4] > 1 and (u[2] - v[2]) % u[4])
+
+    def need(q, sem, val):
+        if seen[q].get(sem, 0) < val:
+            eng[q].wait_ge(T.sem[sem], val)
+            seen[q][sem] = val
+
+    def order(q, reads, writes, free=()):
+        for kind, views in (("r", reads), ("w", writes)):
+            for v in views:
+                ps = v[1][:2] == "ps"
+                for k, u, uq, sem, val in log.get(v[1], ()):
+                    if ps:
+                        hit = uq != q or ((kind, k) != ("r", "r") and (kind == "r" or k == "r" or v[1] not in free))
+                    else:
+                        hit = (kind, k) != ("r", "r") and clash(v, u)
+                    if hit:
+                        need(q, sem, val)
+
+    def note(q, reads, writes, sem, val):
+        for v in writes:
+            old = log.get(v[1], [])
+            keep = [e for e in old if not (v[1][:2] == "ps" or (v[4] == 1 and v[2] <= e[1][2] and e[1][3] <= v[3])
+                                           or (v[4] == e[1][4] and v[2] == e[1][2] and v[3] == e[1][3]))]
+            log[v[1]] = keep + [("w", v, q, sem, val)]
+        for v in reads:
+            log.setdefault(v[1], []).append(("r", v, q, sem, val))
+
+    def run(q, fn, outs, ins, free=()):
+        order(q, ins, outs, free)
+        cnt[q] += 1
+        fn(eng[q]).then_inc(T.sem[q], 1)
+        note(q, ins, outs, q, cnt[q])
+
+    def dma(q, out, in_, outs, ins):
+        order(q, ins, outs)
+        sem = "d%d" % ndma[0]
+        ndma[0] += 1
+        eng[q].dma_start(out, in_).then_inc(T.sem[sem], 16)
+        final[sem] = 16
+        note(q, ins, outs, sem, 16)
+
+    def ts(out, a, s1, s2, op0, op1=None):
+        ins = [a] + [s for s in (s1, s2) if isinstance(s, tuple)]
+        v1, v2 = [s[0] if isinstance(s, tuple) else s for s in (s1, s2)]
+        if op1 is None:
+            run("V", lambda e: e.tensor_scalar(out[0], a[0], v1, None, op0), [out], ins)
+        else:
+            run("V", lambda e: e.tensor_scalar(out[0], a[0], v1, v2, op0, op1), [out], ins)
+
+    def tt(out, a, b, op):
+        run("V", lambda e: e.tensor_tensor(out[0], a[0], b[0], op), [out], [a, b])
+
+    def cp(out, a):
+        run("V", lambda e: e.tensor_copy(out[0], a[0]), [out], [a])
+
+    def scan(out, a, b, init, op0, op1):
+        run("V", lambda e: e.tensor_tensor_scan(out[0], a[0], b[0], init, op0, op1), [out], [a, b])
+
+    def fill(out, c):
+        run("V", lambda e: e.memset(out[0], c), [out], [])
+
+    def quant(code, a, n, tile):
+        run("V", lambda e: e.quantize_mx(T[code][:, a:a + n], T[code + "S"][:, a:a + n], tile[0]),
+            [B(code, a, a + n), B(code + "S", a, a + n)], [tile])
+
+    def act(out, a, func=AF.Copy, scale=1.0, bias=None, accum=None):
+        ins = [a] + [s for s in (scale,) if isinstance(s, tuple)]
+        outs = [out] + ([accum] if accum is not None else [])
+        kw = {}
+        if bias is not None:
+            kw["bias"] = bias
+        if isinstance(scale, tuple):
+            kw["scale"] = scale[0]
+        elif scale != 1.0:
+            kw["scale"] = scale
+        if accum is not None:
+            kw["accum_out"] = accum[0]
+        run("A", lambda e: e.activation(out[0], a[0], func, **kw), outs, ins)
+
+    def mm(bank, n, st, a, mvg, b, start=True, stop=True):
+        name = "ps%d" % bank
+        run("P", lambda e: e.matmul_mx(T[name][:, 0:n], T[st][:, a:a + 128], T[st + "S"][:, a:a + 128],
+                                       T[mvg][:, b:b + n], T[mvg + "S"][:, b:b + n], start, stop),
+            [B(name, 0, n)], [B(st, a, a + 128), B(st + "S", a, a + 128), B(mvg, b, b + n), B(mvg + "S", b, b + n)],
+            free=() if start else (name,))
+
+    def gather(q, out, win, off):
+        w = win[0].indirect(off[0])
+        if q == "V":
+            run("V", lambda e: e.tensor_copy(out[0], w), [out], [win, off])
+        else:
+            run("A", lambda e: e.activation(out[0], w, AF.Copy), [out], [win, off])
+
+    def iota(name, pattern, base, cm):
+        out = B(name)
+        if SCRATCH[out[1]][2] != I4:
+            run("G", lambda e: e.iota(out[0], pattern, base, cm, allow_small_or_imprecise_dtypes=True), [out], [])
+        else:
+            run("G", lambda e: e.iota(out[0], pattern, base, cm), [out], [])
+
+    def send(parts, dst, rsem, lsem):
+        engs = topo.engines(core, dst)
+        rid, pid, _s = topo.addr(dst)
+        m = topo.mask(core, dst)
+        order("G", [s for d, s in parts], [])
+        tot = 0
+        for d, s in parts:
+            g.remote_dma(d[0], s[0], T.sem[rsem], T.sem[lsem], pid, rid, m)
+            tot += len(engs)
+        final[lsem] = tot
+        final[rsem] = tot
+        for d, s in parts:
+            note("G", [s], [], lsem, tot)
+            note("R", [], [d], rsem, tot)
+
+    dma("S", T.x0[:], T.x[:], [B("x0")], [])
+    dma("A", T.ut[:], T.u[:], [B("ut")], [])
+    fill(B("zz"), 0.0)
+    iota("iu", [[16, 8]], 0, 0)
+    iota("ip", [[0, 1]], 0, 1)
+    iota("ikp", [[1, 256]], 128, -1)
+    iota("kbi", [[0, 16], [1, 16]], 0, 0)
+    iota("ikf", [[1, 256]], 0, 0)
+    iota("cb0", [[0, 8], [-1024, 2]], 512, 0)
+    iota("cb1", [[0, 4], [-1024, 2], [0, 2]], 512, 0)
+    iota("cb2", [[0, 2], [-1024, 2], [0, 4]], 512, 0)
+    iota("ig8", [[1, 8]], 0, 0)
+    iota("iposf", [[1, 50]], -2, 0)
+    iota("iposi", [[1, 48]], 0, 0)
+    iota("im", [[16, 16]], 0, 0)
+    for name, n in (("cw", 512), ("bt", 1024), ("ebig", 2048), ("rot", 512), ("rt", 512), ("tc", 1536), ("tt", 1024), ("mv", 512)):
+        for lo in range(0, n, 512):
+            dma("S", T[name][:, lo:lo + 512], T.zz[:], [B(name, lo, lo + 512)], [B("zz")])
+    dma("S", T.wq[:].bitcast(dt.uint8), T.wc[:], [B("wq")], [])
+    dma("S", T.wqS[:], T.ws[:], [B("wqS")], [])
+    for b in range(4):
+        dma("S", T.dy[:, 272 * b + 256:272 * b + 272], T.zz[:, 0:16], [B("dy", 272 * b + 256, 272 * b + 272)], [B("zz", 0, 16)])
+
+    cp(B("ul"), B("iu"))
+    pi = lambda k: B("pi", k, k + 1)
+    pf = lambda k: B("pf", k, k + 1)
+    ts(pi(1), B("ip"), 15, None, OP.bitwise_and)
+    ts(pi(2), B("ip"), 7, None, OP.bitwise_and)
+    ts(pi(3), B("ip"), 4, None, OP.arith_shift_right)
+    ts(pi(4), B("ip"), 3, 1, OP.arith_shift_right, OP.bitwise_and)
+    ts(B("kai"), B("ikp"), 15, None, OP.bitwise_and)
+    cp(B("pf", 1, 5), B("pi", 1, 5))
+    ts(B("hd"), B("kbi"), 0.0, BIG, OP.is_equal, OP.mult)
+    ts(B("maskd"), B("kai"), 0.0, BIG, OP.is_gt, OP.mult)
+    ts(B("sg"), B("kbi"), 0.0, None, OP.is_gt)
+    act(B("kk"), B("ikf"), AF.Identity, bias=-127.5)
+    quant("xqa", 0, 256, B("x0"))
+    quant("uq", 0, 128, B("ut"))
+    ul = B("ul")
+    run("V", lambda e: e.tensor_copy(T.ur[:].bitcast(dt.uint32), T.uq[:].bitcast(dt.uint32).indirect(ul[0])), [B("ur")], [B("uq"), ul])
+    run("A", lambda e: e.activation(T.urS[:], T.uqS[:].indirect(ul[0]), AF.Copy), [B("urS")], [B("uqS"), ul])
+
+    def constants_1():
+        for b in range(3):
+            ts(pf(8 + b), pf(1), 1.0 + b, None, OP.is_equal)
+        ts(B("gm"), B("ig8"), pf(3), None, OP.is_equal)
+        for b in range(3):
+            ts(B("cb%d" % b), B("cb%d" % b), pf(8 + b), None, OP.mult)
+        ts(pf(6), pf(4), 500.0 - 1e6, 1e6, OP.mult, OP.add)
+        tt(B("cb0"), B("cb0"), B("cb1"), OP.add)
+        ts(pf(7), pf(4), 999.0, 1.0, OP.mult, OP.add)
+        tt(B("cb0"), B("cb0"), B("cb2"), OP.add)
+        for gg in range(8):
+            act(B("cw", 64 * gg, 64 * gg + 64, 4), B("cb0"), scale=B("gm", gg, gg + 1))
+        ts(B("kz"), B("kk"), pf(4), 1536.0, OP.mult, OP.add)
+
+    def constants_g():
+        for b in range(4):
+            o = B("ebig", 512 * b + b, 512 * b + 512, 4)
+            run("G", lambda e: e.affine_select(o[0], T.zz[:, 0:128], [[1, 128]], OP.not_equal, 32.0, 0, -1), [o], [B("zz", 0, 128)])
+        for t in range(2):
+            o = B("rot", t, 512, 4)
+            run("G", lambda e: e.affine_select(o[0], T.zz[:, 0:128], [[1, 128]], OP.not_equal, 1.0, 16, -1), [o], [B("zz", 0, 128)])
+            run("G", lambda e: e.affine_select(o[0], o[0], [[1, 128]], OP.not_equal, 1.0, -112, -1), [o], [o])
+
+    def constants_2():
+        ts(B("pos2"), B("iposf", 2, 50), 30.5, None, OP.is_gt)
+        ts(B("kai", 0, 48), B("iposi"), 1, None, OP.bitwise_and)
+        ts(pf(11), pf(2), 2.0, None, OP.mult)
+        tt(B("pos3"), B("pos2"), B("kai", 0, 48), OP.max)
+        ts(pf(12), pf(2), -2.0, 30.0, OP.mult, OP.add)
+        ts(B("fbp"), B("pos3"), 1e6, 7936 * EPS, OP.mult, OP.add)
+        ts(pf(13), pf(2), 2.0, 30.0, OP.mult, OP.add)
+        cp(B("fbz"), B("fbp"))
+        ts(B("nega"), B("iposf"), pf(11), None, OP.is_equal)
+        ts(B("fbz", 0, 15, 2), B("fbz", 0, 15, 2), 0.0, None, OP.mult)
+        ts(B("negb"), B("iposf"), pf(12), None, OP.is_equal)
+        ts(B("negc"), B("iposf"), pf(13), None, OP.is_equal)
+        tt(B("nega"), B("nega"), B("negb"), OP.max)
+        ts(pf(14), pf(4), EPS - 512 * EPS, 512 * EPS, OP.mult, OP.add)
+        tt(B("nega"), B("nega"), B("negc"), OP.max)
+        ts(pf(15), pf(4), EPS, None, OP.mult)
+        tt(B("sig"), B("nega", 0, 48), B("nega", 2, 50), OP.subtract)
+        ts(B("wt0"), B("ig8"), pf(3), pf(14), OP.is_equal, OP.mult)
+        ts(B("wt1"), B("ig8"), pf(3), pf(15), OP.is_equal, OP.mult)
+        for c in range(16):
+            pat, o = B("fbz" if c < 2 else "fbp"), B("fb", W * c, W * c + W)
+            dma("S", o[0], pat[0], [o], [pat])
+        dma("S", T.vt[:], T.v[:], [B("vt")], [])
+
+    def constants_3():
+        for gg in range(8):
+            for t in range(2):
+                act(B("tc", 4 * W * gg + t, 4 * W * gg + 4 * W, 4), B("sig"), scale=B("wt%d" % t, gg, gg + 1))
+
+    def constants_4():
+        ts(B("mask16"), B("kai2"), 0.0, None, OP.is_equal)
+        for h in range(2):
+            for d in range(2):
+                ts(B("mv", 32 * h + 2 * h + d, 32 * h + 32, 4), B("ig8"), pf(3), 1.0 / EPS, OP.is_equal, OP.mult)
+        quant("rotq", 0, 128, B("rot"))
+        quant("eq_", 0, 512, B("ebig"))
+        quant("mvq", 0, 128, B("mv"))
+        ts(B("kcol"), B("im"), pf(1), -127.5, OP.add, OP.add)
+
+    TB = ((0, 1), (2, 7))
+    HB = ((3, 4, 5, 6), (0, 1, 2, 7))
+    for r in range(2):
+        dst = T.cores[rank ^ STEP[r]]
+        L = "abc"
+        xq, px, zq, yq, py = "xq" + L[r], "px" + L[r], "zq" + L[r], "yq" + L[r], "py" + L[r]
+        lc, plc = "lc%d" % r, "plc%d" % r
+        send([(U8(B(px)), U8(B(xq))), (B(px + "S"), B(xq + "S"))], dst, "rx%d" % r, "lx%d" % r)
+        if r == 0:
+            constants_g()
+        mm(1, 256, "ur", 0, xq, 0)
+        mm(0, 256, "ur", 0, xq, 0)
+        mm(2, 256, "uq", 0, xq, 0)
+        act(B("ab"), B("ps0", 0, 256), AF.Abs, scale=0.6 * 2.0 ** -23, bias=2.0 ** -122)
+        act(B("lb", 0, 256), B("ps0", 0, 256))
+        act(B("bt", 0, 1024, 4), B("ps2", 0, 256), AF.Sign, bias=-2.0 ** -100)
+        if r == 0:
+            ts(B("kai2"), B("kai", 0, 16), 1.0, None, OP.mult)
+            constants_1()
+        tt(B("sd"), B("ps1", 0, 256), B("maskd"), OP.add)
+        scan(B("sx"), B("hd"), B("sd"), 0.0, OP.add, OP.min)
+        tt(B("lb", 256, 512), B("ps1", 0, 256), B("ab"), OP.add)
+        for m in range(16):
+            ts(B("cm", 256 * m, 256 * m + 256), B("lb", 16 * m + 16, 16 * m + 272), B("sx", 16 * m + 15, 16 * m + 16), None, OP.is_le)
+            act(B("junk", 256 * m, 256 * m + 256), B("cm", 256 * m, 256 * m + 256), AF.Identity, bias=-257 / 512, accum=B("acc", m, m + 1))
+            if m == (5 if r == 0 else 2):
+                if r == 0:
+                    quant("cwq", 0, 128, B("cw"))
+                quant("btq", 0, 256, B("bt"))
+                mm(2, 256, "cwq", 0, "btq", 0)
+            if m == 4 and r == 0:
+                constants_2()
+            if m == 8:
+                tt(B("et"), B("ps1", 0, 256), B("sx"), OP.is_equal)
+            if m == 9:
+                tt(B("z"), B("ps2", 0, 256), B("kz"), OP.add)
+            if m == 10:
+                scan(B("ets"), B("sg"), B("et"), 0.0, OP.mult, OP.add)
+            if m == 12 and r == 0:
+                constants_4()
+        if r == 0:
+            constants_3()
+            quant("tcq", 0, 384, B("tc"))
+        for b in range(4):
+            mm(3 + b, 256, "eq_", 128 * b, px, 0)
+        tt(B("rl"), B("acc"), B("ets", 15, 256, 16), OP.add)
+        ts(B("l1"), B("rl"), 127.5, None, OP.add)
+        ts(B("rt", 0, 64, 4), B("rl"), K16, K16, OP.add, OP.subtract)
+        l1 = B("l1")
+        run("V", lambda e: e.tensor_copy(T.zs[:, 16:272].indirect(l1[0]), T.z[:]), [B("zs", 16, 272)], [B("z"), l1])
+        tt(B("rt", 1, 64, 4), B("rl"), B("rt", 0, 64, 4), OP.subtract)
+        cp(B("zs", 0, 16), B("zs", 256, 272))
+        quant("rtq", 0, 128, B("rt"))
+        mm(7, 128, "rotq", 0, "rtq", 0)
+        ts(B("d0"), B("zs"), pf(6), pf(7), OP.is_lt, OP.mult)
+        ts(B("d1"), B("zs"), K16, K16, OP.add, OP.subtract)
+        scan(B("tb"), B("d0"), B("zs"), 64.0, OP.add, OP.min)
+        scan(B("w0"), B("d0"), B("d1"), 64.0, OP.add, OP.min)
+        ts(B("l2"), B("ps7", 0, 16), 127.5, None, OP.add)
+        tt(B("w1", 16, 272), B("tb", 16, 272), B("w0", 16, 272), OP.subtract)
+        for b in range(4):
+            act(B("fp", 256 * b, 256 * b + 256), B("ps%d" % (3 + b), 0, 256), scale=1 / 32)
+        gather("V", B("tt", 0, 1024, 4), B("w0", 16, 272), B("l2"))
+        gather("A", B("tt", 1, 1024, 4), B("w1", 16, 272), B("l2"))
+        quant("ttq", 0, 256, B("tt"))
+        for b in range(4):
+            mm(3 + b, 256, "eq_", 128 * b, xq, 0)
+        for b in range(4):
+            act(B("fo", 256 * b, 256 * b + 256), B("ps%d" % (3 + b), 0, 256), scale=1 / 32)
+        for k in range(2):
+            for h in range(2):
+                mm(TB[k][h], 4 * W, "ttq", 128 * h, "tcq", 4 * W * k)
+        for b in range(4):
+            mm(HB[0][b], 128, "eq_", 128 * b, xq, 0, True, False)
+        for k in range(8):
+            for h in range(2):
+                c = W * (2 * k + h)
+                scan(B("so", c, c + W - 1), B("ps%d" % TB[k // 4][h], W * (k % 4), W * (k % 4) + W - 1), B("fb", c, c + W - 1), -100.0,
+                     OP.subtract, OP.min)
+            for h in range(2):
+                c = W * (2 * k + h)
+                if k < 7:
+                    tt(B("fb", c + 2 * W, c + 2 * W + 15, 2), B("fb", c, c + 15, 2), B("so", c + 31, c + 46, 2), OP.is_ge)
+            if k in (3, 6, 7):
+                k0 = {3: 0, 6: 4, 7: 7}[k]
+                a, b = 2 * k0, 2 * k + 2
+                ev = B("so", W * a + 46, W * b, W)
+                ts(B("dah", a, b), ev, KE16, KE16, OP.add, OP.subtract)
+                ts(B("dhh", a, b), ev, KE256, KE256, OP.add, OP.subtract)
+                tt(B("ddb", a, b), ev, B("dah", a, b), OP.subtract)
+                tt(B("dda", a, b), B("dah", a, b), B("dhh", a, b), OP.subtract)
+                for kk in range(k0, k + 1):
+                    for d in (1, 0):
+                        for h in range(2):
+                            o = B("ex", 64 * kk + 2 * h + d, 64 * kk + 64, 4)
+                            col = B(("dda", "ddb")[d], 2 * kk + h, 2 * kk + h + 1)
+                            if kk == 7 and h == 1:
+                                ts(o, B("mask16"), col, None, OP.mult)
+                            else:
+                                act(o, B("mask16"), scale=col)
+        quant("exq", 0, 128, B("ex"))
+        mm(7, 128, "exq", 0, "mvq", 0)
+        ts(B(lc), B("ps7", 0, 16), 127.5, None, OP.add)
+        send([(B(plc), B(lc))], dst, "rl%d" % r, "ll%d" % r)
+        for b in range(4):
+            mm(HB[1][b], 128, "eq_", 128 * b, xq, 128, True, False)
+        gather("A", B("crow"), B("kk"), B(lc))
+        if r == 0:
+            fill(B("fz"), 1.0)
+            ts(B("fz", 0, 1024, 256), B("fz", 0, 1024, 256), 0.0, None, OP.mult)
+
+        def equal(q):
+            for m in range(4 * q, 4 * q + 4):
+                ts(B("eq", 256 * m, 256 * m + 256), B("crow"), B("kcol", m, m + 1), None, OP.is_equal)
+
+        def taken(q):
+            scan(B("pm", 1024 * q, 1024 * q + 1024), B("fz"), B("eq", 1024 * q, 1024 * q + 1024), 0.0, OP.mult, OP.max)
+
+        def counted(m0, m1):
+            for m in range(m0, m1):
+                act(B("junk", 256 * m, 256 * m + 256), B("pm", 256 * m, 256 * m + 256), accum=B("acc2", m, m + 1))
+        equal(0)
+        taken(0)
+        counted(0, 2)
+        equal(1)
+        for h in range(2):
+            for b in range(4):
+                gather("VVAA"[b], B("zt", 512 * h + b, 512 * h + 512, 4), B("fp", 256 * b, 256 * b + 256), B(plc, 8 * h, 8 * h + 8))
+            quant(zq, 128 * h, 128, B("zt", 512 * h, 512 * h + 512))
+            for b in range(4):
+                mm(HB[h][b], 128, "wq", 128 * b, zq, 128 * h, False, True)
+        for h in range(2):
+            for b in range(4):
+                o, i = B("yt", 512 * h + b, 512 * h + 512, 4), B("ps%d" % HB[h][b], 0, 128)
+                if b % 2 == 0:
+                    ts(o, i, 0.03125, None, OP.mult)
+                else:
+                    act(o, i, scale=0.03125)
+            quant(yq, 128 * h, 128, B("yt", 512 * h, 512 * h + 512))
+            q = (128 * h, 128 * h + 128)
+            send([(U8(B(py, *q)), U8(B(yq, *q))), (B(py + "S", *q), B(yq + "S", *q))], dst, "ry%d%d" % (r, h), "ly%d%d" % (r, h))
+        taken(1)
+        counted(2, 8)
+        equal(2)
+        taken(2)
+        counted(8, 12)
+        equal(3)
+        taken(3)
+        counted(12, 13)
+        for m in range(13, 16):
+            o, i = B("acc2", m, m + 1), B("pm", 256 * m, 256 * m + 256)
+            run("V", lambda e: e.tensor_reduce(o[0], i[0], AxisListType.X, OP.add), [o], [i])
+        ts(B("l4"), B("acc2"), -1.0, 256.0, OP.mult, OP.add)
+        if r == 1:
+            ts(B("srow"), B("crow"), 127.5, None, OP.add)
+            dma("S", T.src[:], T.srow[0:128:16, :], [], [B("srow")])
+            quant("vq", 0, 128, B("vt"))
+        for h in range(2):
+            for b in range(4):
+                mm(HB[h][b], 128, "eq_", 128 * b, py, 128 * h)
+        for h in range(2):
+            for b in range(4):
+                o, i = B("dy", 272 * b + 128 * h, 272 * b + 128 * h + 128), B("ps%d" % HB[h][b], 0, 128)
+                if b % 2 == 0:
+                    ts(o, i, 1 / 32, None, OP.mult)
+                else:
+                    act(o, i, scale=1 / 32)
+        xn, l4 = "x%d" % (r + 1), B("l4")
+        for b in range(4):
+            win = B("dy", 272 * b, 272 * b + 272)
+            w, o, f = win[0].indirect(l4[0]), B(xn, b, 1024, 4), B("fo", 256 * b, 256 * b + 256)
+            run("V", lambda e: e.tensor_tensor(o[0], w, f[0], OP.add), [o], [win, l4, f])
+        quant("xq" + L[r + 1], 0, 256, B(xn))
+    dma("S", T.oc[:], T.xqc[:].bitcast(dt.uint8), [], [B("xqc")])
+    for k in range(4):
+        dma("A", T.osc[4 * k:4 * k + 4, :], T.xqcS[32 * k:32 * k + 4, :], [], [B("xqcS")])
+    mm(2, 256, "vq", 0, "xqc", 0)
+    cp(B("yout"), B("ps2", 0, 256))
+    dma("S", T.y[:], T.yout[:], [], [B("yout")])
+    for q in ("V", "A", "P", "G"):
+        need("G", q, cnt[q])
+    for sem, val in final.items():
+        need("G", sem, val)

@@ -46,7 +46,7 @@ for _n, _w in (("uq", 128), ("ur", 128), ("vq", 128), ("wq", 512), ("xqa", 256),
 for _k in range(8):
     SCRATCH["ps%d" % _k] = ("psum", [128, 512], F4)
 
-NDMA = 56
+NDMA = 16
 SEMAPHORES = (["V", "A", "P", "G"] + ["d%d" % k for k in range(NDMA)] + [k + "%d" % r for k in ("rx", "lx", "rl", "ll") for r in (0, 1)]
               + [k + "%d%d" % (r, h) for k in ("ry", "ly") for r in (0, 1) for h in (0, 1)])
 
@@ -85,6 +85,7 @@ def rank_program(g, core, T, topo):
             seen[q][sem] = val
 
     def order(q, reads, writes, free=()):
+        wants = {}
         for kind, views in (("r", reads), ("w", writes)):
             for v in views:
                 ps = v[1][:2] == "ps"
@@ -94,7 +95,9 @@ def rank_program(g, core, T, topo):
                     else:
                         hit = (kind, k) != ("r", "r") and clash(v, u)
                     if hit:
-                        need(q, sem, val)
+                        wants[sem] = max(val, wants.get(sem, 0))
+        for sem, val in wants.items():
+            need(q, sem, val)
 
     def note(q, reads, writes, sem, val):
         for v in writes:
@@ -171,12 +174,15 @@ def rank_program(g, core, T, topo):
         else:
             run("A", lambda e: e.activation(out[0], w, AF.Copy), [out], [win, off])
 
-    def iota(name, pattern, base, cm):
-        out = B(name)
+    def iota(out, pattern, base, cm):
+        out = B(out) if isinstance(out, str) else out
         if SCRATCH[out[1]][2] != I4:
             run("G", lambda e: e.iota(out[0], pattern, base, cm, allow_small_or_imprecise_dtypes=True), [out], [])
         else:
             run("G", lambda e: e.iota(out[0], pattern, base, cm), [out], [])
+
+    def mark(out, in_, pattern, fill, base, cm):
+        run("G", lambda e: e.affine_select(out[0], in_[0], pattern, OP.not_equal, fill, base, cm), [out], [in_])
 
     def send(parts, dst, rsem, lsem):
         engs = topo.engines(core, dst)
@@ -208,15 +214,10 @@ def rank_program(g, core, T, topo):
     iota("iposf", [[1, 50]], -2, 0)
     iota("iposi", [[1, 48]], 0, 0)
     iota("im", [[16, 16]], 0, 0)
-    for name, n in (("cw", 512), ("bt", 1024), ("ebig", 2048), ("rot", 512), ("rt", 512), ("tc", 1536), ("tt", 1024), ("mv", 512)):
-        for lo in range(0, n, 512):
-            dma("S", T[name][:, lo:lo + 512], T.zz[:], [B(name, lo, lo + 512)], [B("zz")])
-    dma("S", T.wq[:].bitcast(dt.uint8), T.wc[:], [B("wq")], [])
-    dma("S", T.wqS[:], T.ws[:], [B("wqS")], [])
-    for b in range(4):
-        dma("S", T.dy[:, 272 * b + 256:272 * b + 272], T.zz[:, 0:16], [B("dy", 272 * b + 256, 272 * b + 272)], [B("zz", 0, 16)])
 
     cp(B("ul"), B("iu"))
+    for name in ("cw", "bt", "mv", "rt"):
+        fill(B(name), 0.0)
     pi = lambda k: B("pi", k, k + 1)
     pf = lambda k: B("pf", k, k + 1)
     ts(pi(1), B("ip"), 15, None, OP.bitwise_and)
@@ -235,68 +236,71 @@ def rank_program(g, core, T, topo):
     run("V", lambda e: e.tensor_copy(T.ur[:].bitcast(dt.uint32), T.uq[:].bitcast(dt.uint32).indirect(ul[0])), [B("ur")], [B("uq"), ul])
     run("A", lambda e: e.activation(T.urS[:], T.uqS[:].indirect(ul[0]), AF.Copy), [B("urS")], [B("uqS"), ul])
 
-    def constants_1():
-        for b in range(3):
-            ts(pf(8 + b), pf(1), 1.0 + b, None, OP.is_equal)
-        ts(B("gm"), B("ig8"), pf(3), None, OP.is_equal)
-        for b in range(3):
-            ts(B("cb%d" % b), B("cb%d" % b), pf(8 + b), None, OP.mult)
-        ts(pf(6), pf(4), 500.0 - 1e6, 1e6, OP.mult, OP.add)
-        tt(B("cb0"), B("cb0"), B("cb1"), OP.add)
-        ts(pf(7), pf(4), 999.0, 1.0, OP.mult, OP.add)
-        tt(B("cb0"), B("cb0"), B("cb2"), OP.add)
-        for gg in range(8):
-            act(B("cw", 64 * gg, 64 * gg + 64, 4), B("cb0"), scale=B("gm", gg, gg + 1))
-        ts(B("kz"), B("kk"), pf(4), 1536.0, OP.mult, OP.add)
-
     def constants_g():
         for b in range(4):
-            o = B("ebig", 512 * b + b, 512 * b + 512, 4)
-            run("G", lambda e: e.affine_select(o[0], T.zz[:, 0:128], [[1, 128]], OP.not_equal, 32.0, 0, -1), [o], [B("zz", 0, 128)])
+            mark(B("ebig", 512 * b, 512 * b + 512), B("zz"), [[1, 512]], 32.0, -b, -4)
+        for t in (2, 3):
+            iota(B("tc", t, 1536, 4), [[0, 384]], 0, 0)
         for t in range(2):
             o = B("rot", t, 512, 4)
-            run("G", lambda e: e.affine_select(o[0], T.zz[:, 0:128], [[1, 128]], OP.not_equal, 1.0, 16, -1), [o], [B("zz", 0, 128)])
-            run("G", lambda e: e.affine_select(o[0], o[0], [[1, 128]], OP.not_equal, 1.0, -112, -1), [o], [o])
+            mark(o, B("zz", 0, 128), [[1, 128]], 1.0, 16, -1)
+            mark(o, o, [[1, 128]], 1.0, -112, -1)
+            iota(B("rot", t + 2, 512, 4), [[0, 128]], 0, 0)
+        for t in (2, 3):
+            iota(B("tt", t, 1024, 4), [[0, 256]], 0, 0)
+        for b in range(4):
+            iota(B("dy", 272 * b + 256, 272 * b + 272), [[0, 16]], 0, 0)
 
-    def constants_2():
-        ts(B("pos2"), B("iposf", 2, 50), 30.5, None, OP.is_gt)
-        ts(B("kai", 0, 48), B("iposi"), 1, None, OP.bitwise_and)
-        ts(pf(11), pf(2), 2.0, None, OP.mult)
-        tt(B("pos3"), B("pos2"), B("kai", 0, 48), OP.max)
-        ts(pf(12), pf(2), -2.0, 30.0, OP.mult, OP.add)
-        ts(B("fbp"), B("pos3"), 1e6, 7936 * EPS, OP.mult, OP.add)
-        ts(pf(13), pf(2), 2.0, 30.0, OP.mult, OP.add)
-        cp(B("fbz"), B("fbp"))
-        ts(B("nega"), B("iposf"), pf(11), None, OP.is_equal)
-        ts(B("fbz", 0, 15, 2), B("fbz", 0, 15, 2), 0.0, None, OP.mult)
-        ts(B("negb"), B("iposf"), pf(12), None, OP.is_equal)
-        ts(B("negc"), B("iposf"), pf(13), None, OP.is_equal)
-        tt(B("nega"), B("nega"), B("negb"), OP.max)
-        ts(pf(14), pf(4), EPS - 512 * EPS, 512 * EPS, OP.mult, OP.add)
-        tt(B("nega"), B("nega"), B("negc"), OP.max)
-        ts(pf(15), pf(4), EPS, None, OP.mult)
-        tt(B("sig"), B("nega", 0, 48), B("nega", 2, 50), OP.subtract)
-        ts(B("wt0"), B("ig8"), pf(3), pf(14), OP.is_equal, OP.mult)
-        ts(B("wt1"), B("ig8"), pf(3), pf(15), OP.is_equal, OP.mult)
-        for c in range(16):
-            pat, o = B("fbz" if c < 2 else "fbp"), B("fb", W * c, W * c + W)
-            dma("S", o[0], pat[0], [o], [pat])
-        dma("S", T.vt[:], T.v[:], [B("vt")], [])
+    todo = []
 
-    def constants_3():
+    def later(f, *a, **k):
+        todo.append(lambda: f(*a, **k))
+
+    def constants_v():
+        for b in range(3):
+            later(ts, pf(8 + b), pf(1), 1.0 + b, None, OP.is_equal)
+        later(ts, B("gm"), B("ig8"), pf(3), None, OP.is_equal)
+        for b in range(3):
+            later(ts, B("cb%d" % b), B("cb%d" % b), pf(8 + b), None, OP.mult)
+        later(ts, pf(6), pf(4), 500.0 - 1e6, 1e6, OP.mult, OP.add)
+        later(tt, B("cb0"), B("cb0"), B("cb1"), OP.add)
+        later(ts, pf(7), pf(4), 999.0, 1.0, OP.mult, OP.add)
+        later(tt, B("cb0"), B("cb0"), B("cb2"), OP.add)
+        for gg in range(8):
+            later(act, B("cw", 64 * gg, 64 * gg + 64, 4), B("cb0"), scale=B("gm", gg, gg + 1))
+        later(ts, B("kz"), B("kk"), pf(4), 1536.0, OP.mult, OP.add)
+        later(ts, B("mask16"), B("kai2"), 0.0, None, OP.is_equal)
+        for h in range(2):
+            for d in range(2):
+                later(ts, B("mv", 32 * h + 2 * h + d, 32 * h + 32, 4), B("ig8"), pf(3), 1.0 / EPS, OP.is_equal, OP.mult)
+        later(quant, "mvq", 0, 128, B("mv"))
+        later(ts, B("kcol"), B("im"), pf(1), -127.5, OP.add, OP.add)
+        later(ts, B("pos2"), B("iposf", 2, 50), 30.5, None, OP.is_gt)
+        later(ts, B("kai", 0, 48), B("iposi"), 1, None, OP.bitwise_and)
+        later(ts, pf(11), pf(2), 2.0, None, OP.mult)
+        later(tt, B("pos3"), B("pos2"), B("kai", 0, 48), OP.max)
+        later(ts, pf(12), pf(2), -2.0, 30.0, OP.mult, OP.add)
+        later(ts, B("fbp"), B("pos3"), 1e6, 7936 * EPS, OP.mult, OP.add)
+        later(ts, pf(13), pf(2), 2.0, 30.0, OP.mult, OP.add)
+        later(cp, B("fbz"), B("fbp"))
+        later(ts, B("nega"), B("iposf"), pf(11), None, OP.is_equal)
+        later(ts, B("fbz", 0, 15, 2), B("fbz", 0, 15, 2), 0.0, None, OP.mult)
+        later(ts, B("negb"), B("iposf"), pf(12), None, OP.is_equal)
+        later(ts, B("negc"), B("iposf"), pf(13), None, OP.is_equal)
+        later(tt, B("nega"), B("nega"), B("negb"), OP.max)
+        later(ts, pf(14), pf(4), EPS - 512 * EPS, 512 * EPS, OP.mult, OP.add)
+        later(tt, B("nega"), B("nega"), B("negc"), OP.max)
+        later(ts, pf(15), pf(4), EPS, None, OP.mult)
+        later(tt, B("sig"), B("nega", 0, 48), B("nega", 2, 50), OP.subtract)
+        later(ts, B("wt0"), B("ig8"), pf(3), pf(14), OP.is_equal, OP.mult)
+        later(ts, B("wt1"), B("ig8"), pf(3), pf(15), OP.is_equal, OP.mult)
+
+    def constants_a():
         for gg in range(8):
             for t in range(2):
                 act(B("tc", 4 * W * gg + t, 4 * W * gg + 4 * W, 4), B("sig"), scale=B("wt%d" % t, gg, gg + 1))
-
-    def constants_4():
-        ts(B("mask16"), B("kai2"), 0.0, None, OP.is_equal)
-        for h in range(2):
-            for d in range(2):
-                ts(B("mv", 32 * h + 2 * h + d, 32 * h + 32, 4), B("ig8"), pf(3), 1.0 / EPS, OP.is_equal, OP.mult)
-        quant("rotq", 0, 128, B("rot"))
-        quant("eq_", 0, 512, B("ebig"))
-        quant("mvq", 0, 128, B("mv"))
-        ts(B("kcol"), B("im"), pf(1), -127.5, OP.add, OP.add)
+        for c in range(16):
+            act(B("fb", W * c, W * c + W), B("fbz" if c < 2 else "fbp"))
 
     TB = ((0, 1), (2, 7))
     HB = ((3, 4, 5, 6), (0, 1, 2, 7))
@@ -316,33 +320,34 @@ def rank_program(g, core, T, topo):
         act(B("bt", 0, 1024, 4), B("ps2", 0, 256), AF.Sign, bias=-2.0 ** -100)
         if r == 0:
             ts(B("kai2"), B("kai", 0, 16), 1.0, None, OP.mult)
-            constants_1()
+            constants_v()
         tt(B("sd"), B("ps1", 0, 256), B("maskd"), OP.add)
         scan(B("sx"), B("hd"), B("sd"), 0.0, OP.add, OP.min)
         tt(B("lb", 256, 512), B("ps1", 0, 256), B("ab"), OP.add)
         for m in range(16):
             ts(B("cm", 256 * m, 256 * m + 256), B("lb", 16 * m + 16, 16 * m + 272), B("sx", 16 * m + 15, 16 * m + 16), None, OP.is_le)
             act(B("junk", 256 * m, 256 * m + 256), B("cm", 256 * m, 256 * m + 256), AF.Identity, bias=-257 / 512, accum=B("acc", m, m + 1))
+            for f in todo[:5]:
+                f()
+            del todo[:5]
             if m == (5 if r == 0 else 2):
                 if r == 0:
                     quant("cwq", 0, 128, B("cw"))
                 quant("btq", 0, 256, B("bt"))
                 mm(2, 256, "cwq", 0, "btq", 0)
-            if m == 4 and r == 0:
-                constants_2()
-            if m == 8:
-                tt(B("et"), B("ps1", 0, 256), B("sx"), OP.is_equal)
-            if m == 9:
-                tt(B("z"), B("ps2", 0, 256), B("kz"), OP.add)
-            if m == 10:
-                scan(B("ets"), B("sg"), B("et"), 0.0, OP.mult, OP.add)
-            if m == 12 and r == 0:
-                constants_4()
+        tt(B("et"), B("ps1", 0, 256), B("sx"), OP.is_equal)
+        tt(B("z"), B("ps2", 0, 256), B("kz"), OP.add)
+        scan(B("ets"), B("sg"), B("et"), 0.0, OP.mult, OP.add)
+        for f in todo:
+            f()
+        del todo[:]
         if r == 0:
-            constants_3()
-            quant("tcq", 0, 384, B("tc"))
+            constants_a()
+            quant("eq_", 0, 512, B("ebig"))
+            dma("S", T.wq[:].bitcast(dt.uint8), T.wc[:], [B("wq")], [B("ets")])
+            dma("S", T.wqS[:], T.ws[:], [B("wqS")], [B("ets")])
         for b in range(4):
-            mm(3 + b, 256, "eq_", 128 * b, px, 0)
+            mm(3 + b, 256, "eq_", 128 * b, xq, 0)
         tt(B("rl"), B("acc"), B("ets", 15, 256, 16), OP.add)
         ts(B("l1"), B("rl"), 127.5, None, OP.add)
         ts(B("rt", 0, 64, 4), B("rl"), K16, K16, OP.add, OP.subtract)
@@ -350,6 +355,8 @@ def rank_program(g, core, T, topo):
         run("V", lambda e: e.tensor_copy(T.zs[:, 16:272].indirect(l1[0]), T.z[:]), [B("zs", 16, 272)], [B("z"), l1])
         tt(B("rt", 1, 64, 4), B("rl"), B("rt", 0, 64, 4), OP.subtract)
         cp(B("zs", 0, 16), B("zs", 256, 272))
+        if r == 0:
+            quant("rotq", 0, 128, B("rot"))
         quant("rtq", 0, 128, B("rt"))
         mm(7, 128, "rotq", 0, "rtq", 0)
         ts(B("d0"), B("zs"), pf(6), pf(7), OP.is_lt, OP.mult)
@@ -358,71 +365,80 @@ def rank_program(g, core, T, topo):
         scan(B("w0"), B("d0"), B("d1"), 64.0, OP.add, OP.min)
         ts(B("l2"), B("ps7", 0, 16), 127.5, None, OP.add)
         tt(B("w1", 16, 272), B("tb", 16, 272), B("w0", 16, 272), OP.subtract)
-        for b in range(4):
-            act(B("fp", 256 * b, 256 * b + 256), B("ps%d" % (3 + b), 0, 256), scale=1 / 32)
         gather("V", B("tt", 0, 1024, 4), B("w0", 16, 272), B("l2"))
+        if r == 0:
+            quant("tcq", 0, 384, B("tc"))
         gather("A", B("tt", 1, 1024, 4), B("w1", 16, 272), B("l2"))
-        quant("ttq", 0, 256, B("tt"))
-        for b in range(4):
-            mm(3 + b, 256, "eq_", 128 * b, xq, 0)
         for b in range(4):
             act(B("fo", 256 * b, 256 * b + 256), B("ps%d" % (3 + b), 0, 256), scale=1 / 32)
+        quant("ttq", 0, 256, B("tt"))
         for k in range(2):
             for h in range(2):
                 mm(TB[k][h], 4 * W, "ttq", 128 * h, "tcq", 4 * W * k)
         for b in range(4):
-            mm(HB[0][b], 128, "eq_", 128 * b, xq, 0, True, False)
+            mm(3 + b, 256, "eq_", 128 * b, px, 0)
+
+        def digits(a, b, first):
+            ev = B("so", W * a + 46, W * b, W)
+            if first:
+                ts(B("dah", a, b), ev, KE16, KE16, OP.add, OP.subtract)
+                ts(B("dhh", a, b), ev, KE256, KE256, OP.add, OP.subtract)
+            else:
+                tt(B("ddb", a, b), ev, B("dah", a, b), OP.subtract)
+                tt(B("dda", a, b), B("dah", a, b), B("dhh", a, b), OP.subtract)
+
+        def spread(k0, k1):
+            for kk in range(k0, k1):
+                for d in (1, 0):
+                    for h in range(2):
+                        o = B("ex", 64 * kk + 2 * h + d, 64 * kk + 64, 4)
+                        col = B(("dda", "ddb")[d], 2 * kk + h, 2 * kk + h + 1)
+                        if kk > 5 and h == 1:
+                            ts(o, B("mask16"), col, None, OP.mult)
+                        else:
+                            act(o, B("mask16"), scale=col)
+        batch = {2: (0, 2), 4: (2, 4), 6: (4, 6), 7: (6, 8)}
         for k in range(8):
             for h in range(2):
                 c = W * (2 * k + h)
                 scan(B("so", c, c + W - 1), B("ps%d" % TB[k // 4][h], W * (k % 4), W * (k % 4) + W - 1), B("fb", c, c + W - 1), -100.0,
                      OP.subtract, OP.min)
+            if k in batch:
+                digits(2 * batch[k][0], 2 * batch[k][1], True)
             for h in range(2):
                 c = W * (2 * k + h)
                 if k < 7:
                     tt(B("fb", c + 2 * W, c + 2 * W + 15, 2), B("fb", c, c + 15, 2), B("so", c + 31, c + 46, 2), OP.is_ge)
-            if k in (3, 6, 7):
-                k0 = {3: 0, 6: 4, 7: 7}[k]
-                a, b = 2 * k0, 2 * k + 2
-                ev = B("so", W * a + 46, W * b, W)
-                ts(B("dah", a, b), ev, KE16, KE16, OP.add, OP.subtract)
-                ts(B("dhh", a, b), ev, KE256, KE256, OP.add, OP.subtract)
-                tt(B("ddb", a, b), ev, B("dah", a, b), OP.subtract)
-                tt(B("dda", a, b), B("dah", a, b), B("dhh", a, b), OP.subtract)
-                for kk in range(k0, k + 1):
-                    for d in (1, 0):
-                        for h in range(2):
-                            o = B("ex", 64 * kk + 2 * h + d, 64 * kk + 64, 4)
-                            col = B(("dda", "ddb")[d], 2 * kk + h, 2 * kk + h + 1)
-                            if kk == 7 and h == 1:
-                                ts(o, B("mask16"), col, None, OP.mult)
-                            else:
-                                act(o, B("mask16"), scale=col)
+            if k in batch:
+                digits(2 * batch[k][0], 2 * batch[k][1], False)
+                spread(*batch[k])
+        for b in range(4):
+            act(B("fp", 256 * b, 256 * b + 256), B("ps%d" % (3 + b), 0, 256), scale=1 / 32)
         quant("exq", 0, 128, B("ex"))
         mm(7, 128, "exq", 0, "mvq", 0)
         ts(B(lc), B("ps7", 0, 16), 127.5, None, OP.add)
         send([(B(plc), B(lc))], dst, "rl%d" % r, "ll%d" % r)
-        for b in range(4):
-            mm(HB[1][b], 128, "eq_", 128 * b, xq, 128, True, False)
+        if r == 1:
+            dma("S", T.vt[:], T.v[:], [B("vt")], [B(lc)])
+        for h in range(2):
+            for b in range(4):
+                mm(HB[h][b], 128, "eq_", 128 * b, xq, 128 * h, True, False)
         gather("A", B("crow"), B("kk"), B(lc))
         if r == 0:
             fill(B("fz"), 1.0)
             ts(B("fz", 0, 1024, 256), B("fz", 0, 1024, 256), 0.0, None, OP.mult)
 
-        def equal(q):
+        def taken(q):
             for m in range(4 * q, 4 * q + 4):
                 ts(B("eq", 256 * m, 256 * m + 256), B("crow"), B("kcol", m, m + 1), None, OP.is_equal)
-
-        def taken(q):
             scan(B("pm", 1024 * q, 1024 * q + 1024), B("fz"), B("eq", 1024 * q, 1024 * q + 1024), 0.0, OP.mult, OP.max)
 
         def counted(m0, m1):
             for m in range(m0, m1):
                 act(B("junk", 256 * m, 256 * m + 256), B("pm", 256 * m, 256 * m + 256), accum=B("acc2", m, m + 1))
-        equal(0)
         taken(0)
+        taken(1)
         counted(0, 2)
-        equal(1)
         for h in range(2):
             for b in range(4):
                 gather("VVAA"[b], B("zt", 512 * h + b, 512 * h + 512, 4), B("fp", 256 * b, 256 * b + 256), B(plc, 8 * h, 8 * h + 8))
@@ -439,15 +455,12 @@ def rank_program(g, core, T, topo):
             quant(yq, 128 * h, 128, B("yt", 512 * h, 512 * h + 512))
             q = (128 * h, 128 * h + 128)
             send([(U8(B(py, *q)), U8(B(yq, *q))), (B(py + "S", *q), B(yq + "S", *q))], dst, "ry%d%d" % (r, h), "ly%d%d" % (r, h))
-        taken(1)
         counted(2, 8)
-        equal(2)
         taken(2)
         counted(8, 12)
-        equal(3)
         taken(3)
-        counted(12, 13)
-        for m in range(13, 16):
+        counted(12, 14)
+        for m in range(14, 16):
             o, i = B("acc2", m, m + 1), B("pm", 256 * m, 256 * m + 256)
             run("V", lambda e: e.tensor_reduce(o[0], i[0], AxisListType.X, OP.add), [o], [i])
         ts(B("l4"), B("acc2"), -1.0, 256.0, OP.mult, OP.add)

import numpy as np
from concourse.bass import DstId, RemoteDMATransfer
from concourse.mybir import dt, AluOpType, AxisListType, ActivationFunctionType

OP = AluOpType
AF = ActivationFunctionType
BIG = 8e28
K16 = 201326592.0
EPS = 2.0 ** -19
KE16, KE256 = 384.0, 6144.0
W = 48
STEP = [1, 2]

F4, BF, I4, U2, CODE, U1 = "float32", "bfloat16", "int32", "uint16", "float8_e4m3fn_x4", "uint8"
SCRATCH, PART = {}, {}


def _add(dtype, **bufs):
    for k, n in bufs.items():
        SCRATCH[k] = ("sbuf", [128, n], dtype)


def _pieces(base, dtype, **bufs):
    at = 0
    for k, n in bufs.items():
        PART[k] = (base, at, n)
        at += (n + 15) // 16 * 16
    SCRATCH[base] = ("sbuf", [128, at], dtype)


_add(BF, x0=1024, x1=1024, x2=1024, ut=512, vt=512, zz=512, kk=256, sg=256, cw=512, rot=512, ebig=2048, tc=1536,
     mv=512, bt=1024, zs=272, z=256, d0=272, d1=272, tb=272, w0=272, w1=272, rt=512, tt=1024, ex=512, et=256, ets=256,
     cm=4096, fo=1024, fp=1024, zt=1024, yt=1024, dy=1088, crow=256, eq=4096, pm=4096, fz=1024)
_add(F4, ikf=256, maskd=256, hd=256, kz=256, kbi=256, lb=512, ab=256, sd=256, sx=256, junk=4096, fb=16 * W, so=16 * W,
     srow=256, yout=256)
_pieces("f4s", F4, pf=16, mask16=16, kcol=16, cb0=16, cb1=16, cb2=16, gm=8, ig8=8, iposf=50, nega=50, negb=50, negc=50, sig=48,
        wt0=8, wt1=8, pos2=48, pos3=48, fbp=48, fbz=48, kai2=16, acc=16, acc2=16, rl=16, dah=16, dhh=16, ddb=16, dda=16)
_pieces("i4s", I4, ip=1, pi=8, ikp=256, iposi=48, iu=8, kai=256, im=16)
_pieces("u2s", U2, ul=8, l1=16, l2=16, l4=16)
_add(U2, lc0=16, lc1=16, plc0=16, plc1=16)
for _n, _w in (("uq", 128), ("ur", 128), ("vq", 128), ("wq", 512), ("xqa", 256), ("xqb", 256), ("xqc", 256), ("pxa", 256), ("pxb", 256),
               ("cwq", 128), ("rotq", 128), ("eq_", 512), ("tcq", 384), ("mvq", 128), ("btq", 256), ("rtq", 128), ("ttq", 256),
               ("exq", 128), ("zqa", 256), ("zqb", 256), ("yqa", 256), ("yqb", 256), ("pya", 256), ("pyb", 256)):
    SCRATCH[_n] = ("sbuf", [128, _w], CODE)
    SCRATCH[_n + "S"] = ("sbuf", [128, _w], U1)
for _k in range(8):
    SCRATCH["ps%d" % _k] = ("psum", [128, 512], F4)

NDMA = 16
SEMAPHORES = (["V", "A", "P", "G"] + ["d%d" % k for k in range(NDMA)] + [k + "%d" % r for k in ("rx", "lx", "rl", "ll") for r in (0, 1)]
              + [k + "%d%d" % (r, h) for k in ("ry", "ly") for r in (0, 1) for h in (0, 1)])


def rank_program(g, core, T, topo):
    rank = T.rank_of(core)
    if rank is None:
        return
    eng = {"V": g.vector, "A": g.scalar, "P": g.tensor, "G": g, "S": g.sync}
    cnt = {"V": 0, "A": 0, "P": 0, "G": 0}
    seen = {q: {} for q in eng}
    log = {}
    ndma = [0]
    final = {}

    def B(name, a=0, b=None, s=1):
        if name in PART:
            base, at, n = PART[name]
            name, a, b = base, a + at, at + (n if b is None else b)
        elif b is None:
            b = SCRATCH[name][1][1]
        ap = T[name][:, a:b] if s == 1 else T[name][:, a:b:s]
        return (ap, name, a, b, s)

    def U8(v):
        return (v[0].bitcast(dt.uint8),) + v[1:]

    def clash(u, v):
        if u[3] <= v[2] or v[3] <= u[2]:
            return False
        return not (u[4] == v[4] > 1 and (u[2] - v[2]) % u[4])

    def need(q, sem, val):
        if seen[q].get(sem, 0) < val:
            eng[q].wait_ge(T.sem[sem], val)
            seen[q][sem] = val

    def order(q, reads, writes, free=()):
        wants = {}
        for kind, views in (("r", reads), ("w", writes)):
            for v in views:
                ps = v[1][:2] == "ps"
                for k, u, uq, sem, val in log.get(v[1], ()):
                    if ps:
                        hit = uq != q or ((kind, k) != ("r", "r") and (kind == "r" or k == "r" or v[1] not in free))
                    else:
                        hit = (kind, k) != ("r", "r") and clash(v, u)
                    if hit:
                        wants[sem] = max(val, wants.get(sem, 0))
        for sem, val in wants.items():
            need(q, sem, val)

    def note(q, reads, writes, sem, val):
        for v in writes:
            old = log.get(v[1], [])
            keep = [e for e in old if not (v[1][:2] == "ps" or (v[4] == 1 and v[2] <= e[1][2] and e[1][3] <= v[3])
                                           or (v[4] == e[1][4] and v[2] == e[1][2] and v[3] == e[1][3]))]
            log[v[1]] = keep + [("w", v, q, sem, val)]
        for v in reads:
            log.setdefault(v[1], []).append(("r", v, q, sem, val))

    def run(q, fn, outs, ins, free=()):
        order(q, ins, outs, free)
        cnt[q] += 1
        fn(eng[q]).then_inc(T.sem[q], 1)
        note(q, ins, outs, q, cnt[q])

    def dma(q, out, in_, outs, ins):
        order(q, ins, outs)
        sem = "d%d" % ndma[0]
        ndma[0] += 1
        eng[q].dma_start(out, in_).then_inc(T.sem[sem], 16)
        final[sem] = 16
        note(q, ins, outs, sem, 16)

    def ts(out, a, s1, s2, op0, op1=None):
        ins = [a] + [s for s in (s1, s2) if isinstance(s, tuple)]
        v1, v2 = [s[0] if isinstance(s, tuple) else s for s in (s1, s2)]
        if op1 is None:
            run("V", lambda e: e.tensor_scalar(out[0], a[0], v1, None, op0), [out], ins)
        else:
            run("V", lambda e: e.tensor_scalar(out[0], a[0], v1, v2, op0, op1), [out], ins)

    def tt(out, a, b, op):
        run("V", lambda e: e.tensor_tensor(out[0], a[0], b[0], op), [out], [a, b])

    def cp(out, a):
        run("V", lambda e: e.tensor_copy(out[0], a[0]), [out], [a])

    def scan(out, a, b, init, op0, op1):
        run("V", lambda e: e.tensor_tensor_scan(out[0], a[0], b[0], init, op0, op1), [out], [a, b])

    def fill(out, c):
        run("V", lambda e: e.memset(out[0], c), [out], [])

    def quant(code, a, n, tile):
        run("V", lambda e: e.quantize_mx(T[code][:, a:a + n], T[code + "S"][:, a:a + n], tile[0]),
            [B(code, a, a + n), B(code + "S", a, a + n)], [tile])

    def act(out, a, func=AF.Copy, scale=1.0, bias=None, accum=None):
        ins = [a] + [s for s in (scale,) if isinstance(s, tuple)]
        outs = [out] + ([accum] if accum is not None else [])
        kw = {}
        if bias is not None:
            kw["bias"] = bias
        if isinstance(scale, tuple):
            kw["scale"] = scale[0]
        elif scale != 1.0:
            kw["scale"] = scale
        if accum is not None:
            kw["accum_out"] = accum[0]
        run("A", lambda e: e.activation(out[0], a[0], func, **kw), outs, ins)

    def mm(bank, n, st, a, mvg, b, start=True, stop=True):
        name = "ps%d" % bank
        run("P", lambda e: e.matmul_mx(T[name][:, 0:n], T[st][:, a:a + 128], T[st + "S"][:, a:a + 128],
                                       T[mvg][:, b:b + n], T[mvg + "S"][:, b:b + n], start, stop),
            [B(name, 0, n)], [B(st, a, a + 128), B(st + "S", a, a + 128), B(mvg, b, b + n), B(mvg + "S", b, b + n)],
            free=() if start else (name,))

    def gather(q, out, win, off):
        w = win[0].indirect(off[0])
        if q == "V":
            run("V", lambda e: e.tensor_copy(out[0], w), [out], [win, off])
        else:
            run("A", lambda e: e.activation(out[0], w, AF.Copy), [out], [win, off])

    def iota(out, pattern, base, cm):
        out = B(out) if isinstance(out, str) else out
        if SCRATCH[out[1]][2] != I4:
            run("G", lambda e: e.iota(out[0], pattern, base, cm, allow_small_or_imprecise_dtypes=True), [out], [])
        else:
            run("G", lambda e: e.iota(out[0], pattern, base, cm), [out], [])

    def mark(out, in_, pattern, fill, base, cm):
        run("G", lambda e: e.affine_select(out[0], in_[0], pattern, OP.not_equal, fill, base, cm), [out], [in_])

    def send(parts, dst, rsem, lsem):
        engs = topo.engines(core, dst)
        rid, pid, _s = topo.addr(dst)
        m = topo.mask(core, dst)
        order("G", [s for d, s in parts], [])
        tot = 0
        for d, s in parts:
            g.remote_dma(d[0], s[0], T.sem[rsem], T.sem[lsem], pid, rid, m)
            tot += len(engs)
        final[lsem] = tot
        final[rsem] = tot
        for d, s in parts:
            note("G", [s], [], lsem, tot)
            note("R", [], [d], rsem, tot)

    dma("S", T.x0[:], T.x[:], [B("x0")], [])
    dma("A", T.ut[:], T.u[:], [B("ut")], [])
    fill(B("zz"), 0.0)
    iota("iu", [[16, 8]], 0, 0)
    iota("ip", [[0, 1]], 0, 1)
    iota("ikp", [[1, 256]], 128, -1)
    iota("kbi", [[0, 16], [1, 16]], 0, 0)
    iota("ikf", [[1, 256]], 0, 0)
    iota("cb0", [[0, 8], [-1024, 2]], 512, 0)
    iota("cb1", [[0, 4], [-1024, 2], [0, 2]], 512, 0)
    iota("cb2", [[0, 2], [-1024, 2], [0, 4]], 512, 0)
    iota("ig8", [[1, 8]], 0, 0)
    iota("iposf", [[1, 50]], -2, 0)
    iota("iposi", [[1, 48]], 0, 0)
    iota("im", [[16, 16]], 0, 0)

    cp(B("ul"), B("iu"))
    for name in ("cw", "bt", "mv", "rt"):
        fill(B(name), 0.0)
    pi = lambda k: B("pi", k, k + 1)
    pf = lambda k: B("pf", k, k + 1)
    ts(pi(1), B("ip"), 15, None, OP.bitwise_and)
    ts(pi(2), B("ip"), 7, None, OP.bitwise_and)
    ts(pi(3), B("ip"), 4, None, OP.arith_shift_right)
    ts(pi(4), B("ip"), 3, 1, OP.arith_shift_right, OP.bitwise_and)
    ts(B("kai"), B("ikp"), 15, None, OP.bitwise_and)
    cp(B("pf", 1, 5), B("pi", 1, 5))
    ts(B("hd"), B("kbi"), 0.0, BIG, OP.is_equal, OP.mult)
    ts(B("maskd"), B("kai"), 0.0, BIG, OP.is_gt, OP.mult)
    ts(B("sg"), B("kbi"), 0.0, None, OP.is_gt)
    act(B("kk"), B("ikf"), AF.Identity, bias=-127.5)
    quant("xqa", 0, 256, B("x0"))
    quant("uq", 0, 128, B("ut"))
    ul = B("ul")
    run("V", lambda e: e.tensor_copy(T.ur[:].bitcast(dt.uint32), T.uq[:].bitcast(dt.uint32).indirect(ul[0])), [B("ur")], [B("uq"), ul])
    run("A", lambda e: e.activation(T.urS[:], T.uqS[:].indirect(ul[0]), AF.Copy), [B("urS")], [B("uqS"), ul])

    def constants_g():
        for b in range(4):
            mark(B("ebig", 512 * b, 512 * b + 512), B("zz"), [[1, 512]], 32.0, -b, -4)
        for t in (2, 3):
            iota(B("tc", t, 1536, 4), [[0, 384]], 0, 0)
        for t in range(2):
            o = B("rot", t, 512, 4)
            mark(o, B("zz", 0, 128), [[1, 128]], 1.0, 16, -1)
            mark(o, o, [[1, 128]], 1.0, -112, -1)
            iota(B("rot", t + 2, 512, 4), [[0, 128]], 0, 0)
        for t in (2, 3):
            iota(B("tt", t, 1024, 4), [[0, 256]], 0, 0)
        for b in range(4):
            iota(B("dy", 272 * b + 256, 272 * b + 272), [[0, 16]], 0, 0)

    todo = []

    def later(f, *a, **k):
        todo.append(lambda: f(*a, **k))

    def constants_v():
        for b in range(3):
            later(ts, pf(8 + b), pf(1), 1.0 + b, None, OP.is_equal)
        later(ts, B("gm"), B("ig8"), pf(3), None, OP.is_equal)
        for b in range(3):
            later(ts, B("cb%d" % b), B("cb%d" % b), pf(8 + b), None, OP.mult)
        later(ts, pf(6), pf(4), 500.0 - 1e6, 1e6, OP.mult, OP.add)
        later(tt, B("cb0"), B("cb0"), B("cb1"), OP.add)
        later(ts, pf(7), pf(4), 999.0, 1.0, OP.mult, OP.add)
        later(tt, B("cb0"), B("cb0"), B("cb2"), OP.add)
        for gg in range(8):
            later(act, B("cw", 64 * gg, 64 * gg + 64, 4), B("cb0"), scale=B("gm", gg, gg + 1))
        later(ts, B("kz"), B("kk"), pf(4), 1536.0, OP.mult, OP.add)
        later(ts, B("mask16"), B("kai2"), 0.0, None, OP.is_equal)
        for h in range(2):
            for d in range(2):
                later(ts, B("mv", 32 * h + 2 * h + d, 32 * h + 32, 4), B("ig8"), pf(3), 1.0 / EPS, OP.is_equal, OP.mult)
        later(quant, "mvq", 0, 128, B("mv"))
        later(ts, B("kcol"), B("im"), pf(1), -127.5, OP.add, OP.add)
        later(ts, B("pos2"), B("iposf", 2, 50), 30.5, None, OP.is_gt)
        later(ts, B("kai", 0, 48), B("iposi"), 1, None, OP.bitwise_and)
        later(ts, pf(11), pf(2), 2.0, None, OP.mult)
        later(tt, B("pos3"), B("pos2"), B("kai", 0, 48), OP.max)
        later(ts, pf(12), pf(2), -2.0, 30.0, OP.mult, OP.add)
        later(ts, B("fbp"), B("pos3"), 1e6, 7936 * EPS, OP.mult, OP.add)
        later(ts, pf(13), pf(2), 2.0, 30.0, OP.mult, OP.add)
        later(cp, B("fbz"), B("fbp"))
        later(ts, B("nega"), B("iposf"), pf(11), None, OP.is_equal)
        later(ts, B("fbz", 0, 15, 2), B("fbz", 0, 15, 2), 0.0, None, OP.mult)
        later(ts, B("negb"), B("iposf"), pf(12), None, OP.is_equal)
        later(ts, B("negc"), B("iposf"), pf(13), None, OP.is_equal)
        later(tt, B("nega"), B("nega"), B("negb"), OP.max)
        later(ts, pf(14), pf(4), EPS - 512 * EPS, 512 * EPS, OP.mult, OP.add)
        later(tt, B("nega"), B("nega"), B("negc"), OP.max)
        later(ts, pf(15), pf(4), EPS, None, OP.mult)
        later(tt, B("sig"), B("nega", 0, 48), B("nega", 2, 50), OP.subtract)
        later(ts, B("wt0"), B("ig8"), pf(3), pf(14), OP.is_equal, OP.mult)
        later(ts, B("wt1"), B("ig8"), pf(3), pf(15), OP.is_equal, OP.mult)

    def constants_a():
        for gg in range(8):
            for t in range(2):
                act(B("tc", 4 * W * gg + t, 4 * W * gg + 4 * W, 4), B("sig"), scale=B("wt%d" % t, gg, gg + 1))
        for c in range(16):
            act(B("fb", W * c, W * c + W), B("fbz" if c < 2 else "fbp"))

    TB = ((0, 1), (2, 7))
    HB = ((3, 4, 5, 6), (0, 1, 2, 7))
    for r in range(2):
        dst = T.cores[rank ^ STEP[r]]
        L = "abc"
        xq, px, zq, yq, py = "xq" + L[r], "px" + L[r], "zq" + L[r], "yq" + L[r], "py" + L[r]
        lc, plc = "lc%d" % r, "plc%d" % r
        send([(U8(B(px)), U8(B(xq))), (B(px + "S"), B(xq + "S"))], dst, "rx%d" % r, "lx%d" % r)
        if r == 0:
            constants_g()
        mm(1, 256, "ur", 0, xq, 0)
        mm(0, 256, "ur", 0, xq, 0)
        mm(2, 256, "uq", 0, xq, 0)
        act(B("ab"), B("ps0", 0, 256), AF.Abs, scale=0.6 * 2.0 ** -23, bias=2.0 ** -122)
        act(B("lb", 0, 256), B("ps0", 0, 256))
        act(B("bt", 0, 1024, 4), B("ps2", 0, 256), AF.Sign, bias=-2.0 ** -100)
        if r == 0:
            ts(B("kai2"), B("kai", 0, 16), 1.0, None, OP.mult)
            constants_v()
        tt(B("sd"), B("ps1", 0, 256), B("maskd"), OP.add)
        scan(B("sx"), B("hd"), B("sd"), 0.0, OP.add, OP.min)
        tt(B("lb", 256, 512), B("ps1", 0, 256), B("ab"), OP.add)
        for m in range(16):
            ts(B("cm", 256 * m, 256 * m + 256), B("lb", 16 * m + 16, 16 * m + 272), B("sx", 16 * m + 15, 16 * m + 16), None, OP.is_le)
            act(B("junk", 256 * m, 256 * m + 256), B("cm", 256 * m, 256 * m + 256), AF.Identity, bias=-257 / 512, accum=B("acc", m, m + 1))
            for f in todo[:5]:
                f()
            del todo[:5]
            if m == (5 if r == 0 else 2):
                if r == 0:
                    quant("cwq", 0, 128, B("cw"))
                quant("btq", 0, 256, B("bt"))
                mm(2, 256, "cwq", 0, "btq", 0)
        tt(B("et"), B("ps1", 0, 256), B("sx"), OP.is_equal)
        tt(B("z"), B("ps2", 0, 256), B("kz"), OP.add)
        scan(B("ets"), B("sg"), B("et"), 0.0, OP.mult, OP.add)
        for f in todo:
            f()
        del todo[:]
        if r == 0:
            constants_a()
            quant("eq_", 0, 512, B("ebig"))
            dma("S", T.wq[:].bitcast(dt.uint8), T.wc[:], [B("wq")], [B("ets")])
            dma("S", T.wqS[:], T.ws[:], [B("wqS")], [B("ets")])
        for b in range(4):
            mm(3 + b, 256, "eq_", 128 * b, xq, 0)
        tt(B("rl"), B("acc"), B("ets", 15, 256, 16), OP.add)
        ts(B("l1"), B("rl"), 127.5, None, OP.add)
        ts(B("rt", 0, 64, 4), B("rl"), K16, K16, OP.add, OP.subtract)
        l1 = B("l1")
        run("V", lambda e: e.tensor_copy(T.zs[:, 16:272].indirect(l1[0]), T.z[:]), [B("zs", 16, 272)], [B("z"), l1])
        tt(B("rt", 1, 64, 4), B("rl"), B("rt", 0, 64, 4), OP.subtract)
        cp(B("zs", 0, 16), B("zs", 256, 272))
        if r == 0:
            quant("rotq", 0, 128, B("rot"))
        quant("rtq", 0, 128, B("rt"))
        mm(7, 128, "rotq", 0, "rtq", 0)
        ts(B("d0"), B("zs"), pf(6), pf(7), OP.is_lt, OP.mult)
        ts(B("d1"), B("zs"), K16, K16, OP.add, OP.subtract)
        scan(B("tb"), B("d0"), B("zs"), 64.0, OP.add, OP.min)
        scan(B("w0"), B("d0"), B("d1"), 64.0, OP.add, OP.min)
        ts(B("l2"), B("ps7", 0, 16), 127.5, None, OP.add)
        tt(B("w1", 16, 272), B("tb", 16, 272), B("w0", 16, 272), OP.subtract)
        gather("V", B("tt", 0, 1024, 4), B("w0", 16, 272), B("l2"))
        if r == 0:
            quant("tcq", 0, 384, B("tc"))
        gather("A", B("tt", 1, 1024, 4), B("w1", 16, 272), B("l2"))
        for b in range(4):
            act(B("fo", 256 * b, 256 * b + 256), B("ps%d" % (3 + b), 0, 256), scale=1 / 32)
        quant("ttq", 0, 256, B("tt"))
        for k in range(2):
            for h in range(2):
                mm(TB[k][h], 4 * W, "ttq", 128 * h, "tcq", 4 * W * k)
        for b in range(4):
            mm(3 + b, 256, "eq_", 128 * b, px, 0)

        def digits(a, b, first):
            ev = B("so", W * a + 46, W * b, W)
            if first:
                ts(B("dah", a, b), ev, KE16, KE16, OP.add, OP.subtract)
                ts(B("dhh", a, b), ev, KE256, KE256, OP.add, OP.subtract)
            else:
                tt(B("ddb", a, b), ev, B("dah", a, b), OP.subtract)
                tt(B("dda", a, b), B("dah", a, b), B("dhh", a, b), OP.subtract)

        def spread(k0, k1):
            for kk in range(k0, k1):
                for d in (1, 0):
                    for h in range(2):
                        o = B("ex", 64 * kk + 2 * h + d, 64 * kk + 64, 4)
                        col = B(("dda", "ddb")[d], 2 * kk + h, 2 * kk + h + 1)
                        if kk > 5 and h == 1:
                            ts(o, B("mask16"), col, None, OP.mult)
                        else:
                            act(o, B("mask16"), scale=col)
        batch = {2: (0, 2), 4: (2, 4), 6: (4, 6), 7: (6, 8)}
        for k in range(8):
            for h in range(2):
                c = W * (2 * k + h)
                scan(B("so", c, c + W - 1), B("ps%d" % TB[k // 4][h], W * (k % 4), W * (k % 4) + W - 1), B("fb", c, c + W - 1), -100.0,
                     OP.subtract, OP.min)
            if k in batch:
                digits(2 * batch[k][0], 2 * batch[k][1], True)
            for h in range(2):
                c = W * (2 * k + h)
                if k < 7:
                    tt(B("fb", c + 2 * W, c + 2 * W + 15, 2), B("fb", c, c + 15, 2), B("so", c + 31, c + 46, 2), OP.is_ge)
            if k in batch:
                digits(2 * batch[k][0], 2 * batch[k][1], False)
                spread(*batch[k])
        for b in range(4):
            act(B("fp", 256 * b, 256 * b + 256), B("ps%d" % (3 + b), 0, 256), scale=1 / 32)
        quant("exq", 0, 128, B("ex"))
        mm(7, 128, "exq", 0, "mvq", 0)
        ts(B(lc), B("ps7", 0, 16), 127.5, None, OP.add)
        send([(B(plc), B(lc))], dst, "rl%d" % r, "ll%d" % r)
        if r == 1:
            dma("S", T.vt[:], T.v[:], [B("vt")], [B(lc)])
        for h in range(2):
            for b in range(4):
                mm(HB[h][b], 128, "eq_", 128 * b, xq, 128 * h, True, False)
        gather("A", B("crow"), B("kk"), B(lc))
        if r == 0:
            fill(B("fz"), 1.0)
            ts(B("fz", 0, 1024, 256), B("fz", 0, 1024, 256), 0.0, None, OP.mult)

        def taken(q):
            for m in range(4 * q, 4 * q + 4):
                ts(B("eq", 256 * m, 256 * m + 256), B("crow"), B("kcol", m, m + 1), None, OP.is_equal)
            scan(B("pm", 1024 * q, 1024 * q + 1024), B("fz"), B("eq", 1024 * q, 1024 * q + 1024), 0.0, OP.mult, OP.max)

        def counted(m0, m1):
            for m in range(m0, m1):
                act(B("junk", 256 * m, 256 * m + 256), B("pm", 256 * m, 256 * m + 256), accum=B("acc2", m, m + 1))
        taken(0)
        taken(1)
        counted(0, 2)
        for h in range(2):
            for b in range(4):
                gather("VVAA"[b], B("zt", 512 * h + b, 512 * h + 512, 4), B("fp", 256 * b, 256 * b + 256), B(plc, 8 * h, 8 * h + 8))
            quant(zq, 128 * h, 128, B("zt", 512 * h, 512 * h + 512))
            for b in range(4):
                mm(HB[h][b], 128, "wq", 128 * b, zq, 128 * h, False, True)
        for h in range(2):
            for b in range(4):
                o, i = B("yt", 512 * h + b, 512 * h + 512, 4), B("ps%d" % HB[h][b], 0, 128)
                if b % 2 == 0:
                    ts(o, i, 0.03125, None, OP.mult)
                else:
                    act(o, i, scale=0.03125)
            quant(yq, 128 * h, 128, B("yt", 512 * h, 512 * h + 512))
            q = (128 * h, 128 * h + 128)
            send([(U8(B(py, *q)), U8(B(yq, *q))), (B(py + "S", *q), B(yq + "S", *q))], dst, "ry%d%d" % (r, h), "ly%d%d" % (r, h))
        counted(2, 8)
        taken(2)
        counted(8, 12)
        taken(3)
        counted(12, 14)
        for m in range(14, 16):
            o, i = B("acc2", m, m + 1), B("pm", 256 * m, 256 * m + 256)
            run("V", lambda e: e.tensor_reduce(o[0], i[0], AxisListType.X, OP.add), [o], [i])
        ts(B("l4"), B("acc2"), -1.0, 256.0, OP.mult, OP.add)
        if r == 1:
            ts(B("srow"), B("crow"), 127.5, None, OP.add)
            dma("S", T.src[:], T.srow[0:128:16, :], [], [B("srow")])
            quant("vq", 0, 128, B("vt"))
        for h in range(2):
            for b in range(4):
                mm(HB[h][b], 128, "eq_", 128 * b, py, 128 * h)
        for h in range(2):
            for b in range(4):
                o, i = B("dy", 272 * b + 128 * h, 272 * b + 128 * h + 128), B("ps%d" % HB[h][b], 0, 128)
                if b % 2 == 0:
                    ts(o, i, 1 / 32, None, OP.mult)
                else:
                    act(o, i, scale=1 / 32)
        xn, l4 = "x%d" % (r + 1), B("l4")
        for b in range(4):
            win = B("dy", 272 * b, 272 * b + 272)
            w, o, f = win[0].indirect(l4[0]), B(xn, b, 1024, 4), B("fo", 256 * b, 256 * b + 256)
            run("V", lambda e: e.tensor_tensor(o[0], w, f[0], OP.add), [o], [win, l4, f])
        quant("xq" + L[r + 1], 0, 256, B(xn))
    dma("S", T.oc[:], T.xqc[:].bitcast(dt.uint8), [], [B("xqc")])
    for k in range(4):
        dma("A", T.osc[4 * k:4 * k + 4, :], T.xqcS[32 * k:32 * k + 4, :], [], [B("xqcS")])
    mm(2, 256, "vq", 0, "xqc", 0)
    cp(B("yout"), B("ps2", 0, 256))
    dma("S", T.y[:], T.yout[:], [], [B("yout")])
    for q in ("V", "A", "P", "G"):
        need("G", q, cnt[q])
    for sem, val in final.items():
        need("G", sem, val)
